import numpy as np
import ml_dtypes


def mxq(x, axis, fmt="e4m3"):
    dtype, down = {"e4m3": (ml_dtypes.float8_e4m3fn, 7), "e5m2": (ml_dtypes.float8_e5m2, 14)}[fmt]
    v = np.moveaxis(np.asarray(x, np.float32).astype(ml_dtypes.bfloat16).astype(np.float64), axis, -1)
    blocks = v.reshape(v.shape[:-1] + (-1, 32))
    amax = np.abs(blocks).max(-1, keepdims=True)
    byte = np.maximum(np.where(amax > 0, np.frexp(amax)[1] - 1 + 127, 0) - down, 1)
    scale = np.exp2(byte - 127.0)
    codes = (blocks / scale).astype(np.float32).astype(dtype).astype(np.float64)
    return np.moveaxis((codes * scale).reshape(v.shape), -1, axis)


WIDE = False


def mx_kscale(k):
    if not WIDE:
        return np.ones(k)
    levels = np.array([10, -10, 5, -5, 0])
    if k % 512:
        return np.exp2(np.random.permutation(np.resize(levels, k // 32))).repeat(32)
    a = np.empty((k // 512, 16))
    for p in range(k // 512):
        a[p, :8] = np.random.permutation(np.resize(levels, 8))
        for g in range(8):
            far = levels[np.abs(levels - a[p, g]) >= 10]
            a[p, g + 8] = far[np.random.randint(len(far))]
    return np.exp2(a.ravel()).repeat(32)


def f64(x):
    return np.asarray(x).astype(np.float64)


def striped(idx):
    return np.tile(np.asarray(idx).reshape(-1, 16).T, (8, 1)).astype(np.uint16)


def unstriped(offs):
    return offs[:16].T.reshape(-1).astype(np.int64)


E2M1 = np.array([0.0, 0.5, 1.0, 1.5, 2.0, 3.0, 4.0, 6.0, -0.0, -0.5, -1.0, -1.5, -2.0, -3.0, -4.0, -6.0])


def pack_weight(w, fmt):
    k, n = w.shape
    w = f64(np.asarray(w, np.float32).astype(ml_dtypes.bfloat16)).reshape(k // 32, 32, n)
    amax = np.abs(w).max(1)
    if fmt == "e4m3":
        byte = np.frexp(amax)[1] - 1 + 127 - 7
    else:
        mant, ex = np.frexp(amax / 6.0)
        byte = np.where(mant > 0.5, ex, ex - 1) + 127
    byte = np.clip(np.where(amax > 0, byte, 1), 1, 254)
    scaled = (w * np.exp2(127.0 - byte)[:, None, :]).reshape(k, n).astype(np.float32)
    by_word = np.ascontiguousarray(scaled.reshape(k // 512, 128, 4, n).transpose(0, 1, 3, 2))
    if fmt == "e4m3":
        words = by_word.astype(ml_dtypes.float8_e4m3fn).view(np.uint8)
    else:
        c = by_word.astype(ml_dtypes.float4_e2m1fn).view(np.uint8) & 0xF
        words = (c[..., 0::2] | (c[..., 1::2] << 4)).reshape(k // 512, 128, 2 * n)
    return np.ascontiguousarray(words), np.ascontiguousarray(byte.astype(np.uint8).reshape(k // 512, 16, n))


def unpack_weight(words, scales, fmt):
    g, _, n = scales.shape
    words = np.ascontiguousarray(words).reshape(g, 128, n, -1)
    if fmt == "e4m3":
        vals = words.view(ml_dtypes.float8_e4m3fn).astype(np.float64)
    else:
        nib = np.empty((g, 128, n, 4), np.uint8)
        nib[..., 0::2] = words & 0xF
        nib[..., 1::2] = words >> 4
        vals = E2M1[nib]
    vals = vals * np.repeat(np.exp2(scales.astype(np.float64) - 127.0), 8, axis=1)[..., None]
    return vals.transpose(0, 1, 3, 2).reshape(g * 512, n)


def sigmoid(v):
    return 1.0 / (1.0 + np.exp(-v))


D, E, T, I, Q, G, B = 512, 512, 2048, 512, 128, 64, 8


def setup_inputs():
    n = np.random.standard_normal
    idx = np.random.permutation(T)[:I]
    fd = mx_kscale(D)
    fe = mx_kscale(E)
    keysp = pack_weight(n((D, T)) / fd[:, None], "e2m1")
    valsp = pack_weight(n((E, T)) / fe[:, None], "e2m1")
    return {
        "query": (n((D, Q)) * 0.8 / np.sqrt(D) * fd[:, None]).astype(np.float32),
        "keys_words": keysp[0],
        "keys_scales": keysp[1],
        "steep": (np.random.uniform(2.0, 8.0, (Q, 1))).astype(np.float32),
        "gout": (n((E, Q)) * 1 / np.sqrt(E) * fe[:, None]).astype(np.float32),
        "vals_words": valsp[0],
        "vals_scales": valsp[1],
        "dquery": (n((D, Q)) * 1.0 / np.sqrt(D) * fd[:, None]).astype(np.float32),
        "base": (0.5 * n((Q, T))).astype(np.float32),
        "offs": striped(idx),
    }


def reference(query, keys_words, keys_scales, steep, gout, vals_words, vals_scales, dquery, base, offs):
    idx = unstriped(offs)
    keysu = unpack_weight(keys_words, keys_scales, "e2m1")
    valsu = unpack_weight(vals_words, vals_scales, "e2m1")
    queryq = mxq(f64(query), 0, "e4m3")
    keysidxg = keysu[:, idx]
    a = queryq.T @ keysidxg
    dqueryq = mxq(f64(dquery), 0, "e4m3")
    ta = dqueryq.T @ keysidxg
    m1 = a.reshape(Q, G, I // G).mean(axis=2)
    m2 = m1.reshape(Q, B, G // B).mean(axis=2)
    mr = np.repeat(m2, G // B, axis=1)
    g1 = sigmoid((m1 - mr) * f64(steep))
    gr = np.repeat(g1, I // G, axis=1)
    p = np.exp(a) * gr
    z = np.sum(p, axis=1, keepdims=True)
    goutq = mxq(f64(gout), 0, "e4m3")
    valsidxg = valsu[:, idx]
    c0 = goutq.T @ valsidxg
    dz = np.sum(c0 * p / np.square(z) * (-1.0), axis=1, keepdims=True)
    dp = c0 / z + dz
    dgr = dp * np.exp(a)
    dg1 = dgr.reshape(Q, G, I // G).sum(axis=2)
    tm1 = ta.reshape(Q, G, I // G).mean(axis=2)
    tm2 = tm1.reshape(Q, B, G // B).mean(axis=2)
    tmr = np.repeat(tm2, G // B, axis=1)
    tg1 = (tm1 - tmr) * f64(steep) * g1 * (1.0 - g1)
    tgr = np.repeat(tg1, I // G, axis=1)
    tp = ta * np.exp(a) * gr + tgr * np.exp(a)
    tz = np.sum(tp, axis=1, keepdims=True)
    tdz = np.sum((tp * c0 - tz * z * 2.0 * c0 * p / np.square(z)) / np.square(z) * (-1.0), axis=1, keepdims=True)
    tdp = tz * c0 / np.square(z) * (-1.0) + tdz
    tdgr = tdp * np.exp(a) + ta * np.exp(a) * dp
    tdg1 = tdgr.reshape(Q, G, I // G).sum(axis=2)
    tdmr = ((tdg1 * g1 + tg1 * dg1) * (1.0 - g1) + tg1 * (-1.0) * dg1 * g1) * f64(steep) * (-1.0)
    tdm2 = tdmr.reshape(Q, B, G // B).sum(axis=2)
    te1 = tdm2 / 8.0
    tr1 = np.repeat(te1, G // B, axis=1)
    tdm1 = ((tdg1 * g1 + tg1 * dg1) * (1.0 - g1) + tg1 * (-1.0) * dg1 * g1) * f64(steep) + tr1
    te2 = tdm1 / 8.0
    tr2 = np.repeat(te2, I // G, axis=1)
    tda = (tdp * gr + tgr * dp) * np.exp(a) + ta * np.exp(a) * dp * gr + tr2
    gs = tda * 512.0
    gf = np.zeros((Q, T))
    gf[:, idx] = gs
    y = f64(base) + gf
    return y

@@ -1,0 +1,207 @@
+import math
+from contextlib import ExitStack
+
+import concourse.mybir as mybir
+
+F32 = mybir.dt.float32
+BF16 = mybir.dt.bfloat16
+I32 = mybir.dt.int32
+U32 = mybir.dt.uint32
+U16 = mybir.dt.uint16
+U8 = mybir.dt.uint8
+FP8X4 = mybir.dt.float8_e4m3fn_x4
+FP4X4 = mybir.dt.float4_e2m1fn_x4
+ALU = mybir.AluOpType
+ACT = mybir.ActivationFunctionType
+AX = mybir.AxisListType
+
+P = 128
+D, T, I, Q, G, B = 512, 2048, 512, 128, 64, 8
+R = I // G
+PACK = 4
+TEMPER = 8.0
+OUT_CHUNKS = 4
+FLOPS = 3 * 2 * D * Q * I
+
+
+def tile_attend_hvblockcontrast_s_kernel(tc, query, keys_words, keys_scales, steep, gout, vals_words, vals_scales, dquery, base, offs, out):
+    nc = tc.nc
+    with ExitStack() as ctx:
+        sb = ctx.enter_context(tc.tile_pool(name="sb", bufs=1))
+        ps = ctx.enter_context(tc.psum_pool(name="ps", bufs=1))
+
+        def small(name, n=G):
+            return sb.tile([P, n], F32, name=name)
+
+        def wide(name):
+            return sb.tile([P, I], F32, name=name)
+
+        def by_group(ap):
+            return ap.rearrange("p (g r) -> p g r", r=R)
+
+        def spread(ap, n):
+            return ap.unsqueeze(2).to_broadcast([P, ap.shape[1], n])
+
+        offsets = sb.tile([P, I // 16], U16, name="offsets")
+        nc.sync.dma_start(offsets[:], offs)
+
+        k_words = sb.tile([P, T], U16, name="k_words")
+        v_words = sb.tile([P, T], U16, name="v_words")
+        k_bytes = sb.tile([P, T], U8, name="k_bytes")
+        v_bytes = sb.tile([P, T], U8, name="v_bytes")
+        window = sb.tile([P, T], F32, name="window")
+        nc.vector.memset(k_bytes[:].bitcast(I32), 0)
+        nc.vector.memset(v_bytes[:].bitcast(I32), 0)
+        nc.vector.memset(window[:], 0.0)
+        warm = small("warm", 8)
+        nc.gpsimd.memset(warm[:], 0.0)
+        warm_out = small("warm_out", 8)
+        nc.scalar.activation(warm_out[:], warm[:], ACT.Exp)
+
+        def load_bytes(tile, src):
+            for quad in range(4):
+                nc.sync.dma_start(tile[32 * quad : 32 * quad + 4, :].bitcast(I32), src[0][4 * quad : 4 * quad + 4, :].bitcast(I32))
+
+        def load_rows(name, src):
+            raw = sb.tile([P, PACK, Q], F32, name=name)
+            nc.sync.dma_start(raw[:], src.rearrange("(p j) w -> p j w", j=PACK))
+            return raw
+
+        nc.sync.dma_start(k_words[:].bitcast(I32), keys_words[0].bitcast(I32))
+        load_bytes(k_bytes, keys_scales)
+        q_raw = load_rows("q_raw", query)
+        dq_raw = load_rows("dq_raw", dquery)
+        nc.sync.dma_start(v_words[:].bitcast(I32), vals_words[0].bitcast(I32))
+        load_bytes(v_bytes, vals_scales)
+        g_raw = load_rows("g_raw", gout)
+        steep_sb = small("steep_sb", 1)
+        nc.sync.dma_start(steep_sb[:], steep)
+        cw = T // OUT_CHUNKS
+        base_sb = sb.tile([P, T], F32, name="base_sb")
+        nc.sync.dma_start(base_sb[:], base)
+
+        qq_bf = sb.tile([P, 2, Q, PACK], BF16, name="qq_bf", align_bytes=64)
+        g_bf = sb.tile([P, Q, PACK], BF16, name="g_bf", align_bytes=64)
+        nc.scalar.copy(qq_bf[:, 0], q_raw[:].rearrange("p j w -> p w j"))
+        nc.scalar.copy(qq_bf[:, 1], dq_raw[:].rearrange("p j w -> p w j"))
+        nc.scalar.copy(g_bf[:], g_raw[:].rearrange("p j w -> p w j"))
+
+        kg_words = sb.tile([P, I], U16, name="kg_words", align_bytes=64)
+        kg_bytes = sb.tile([P, I], U8, name="kg_bytes", align_bytes=64)
+        vg_words = sb.tile([P, I], U16, name="vg_words", align_bytes=64)
+        qq_codes = sb.tile([P, 2 * Q], U32, name="qq_codes", align_bytes=64)
+        qq_scales = sb.tile([P, 2 * Q], U8, name="qq_scales", align_bytes=64)
+        g_codes = sb.tile([P, Q], U32, name="g_codes", align_bytes=64)
+        g_scales = sb.tile([P, Q], U8, name="g_scales", align_bytes=64)
+
+        nc.vector.tensor_copy(kg_words[:], k_words[:].indirect(offsets[:]))
+        nc.vector.tensor_copy(kg_bytes[:], k_bytes[:].indirect(offsets[:]))
+        a = ps.tile([P, I], F32, name="a")
+        ta = ps.tile([P, I], F32, name="ta")
+        c0 = ps.tile([P, I], F32, name="c0")
+        for s, dst in enumerate((a, ta)):
+            cols = slice(s * Q, (s + 1) * Q)
+            nc.vector.quantize_mx(qq_codes[:, cols].bitcast(FP8X4), qq_scales[:, cols], qq_bf[:, s].rearrange("p w j -> p (w j)"))
+            nc.tensor.matmul_mx(dst[:], lhsT=qq_codes[:, cols].bitcast(FP8X4), lhsT_scale=qq_scales[:, cols],
+                                rhs=kg_words[:].bitcast(FP4X4), rhs_scale=kg_bytes[:], start=True, stop=True)
+        nc.vector.tensor_copy(vg_words[:], v_words[:].indirect(offsets[:]))
+        nc.vector.quantize_mx(g_codes[:].bitcast(FP8X4), g_scales[:], g_bf[:].rearrange("p w j -> p (w j)"))
+
+        s16 = small("s16", 1)
+        ns16 = small("ns16", 1)
+        nc.scalar.activation(s16[:], steep_sb[:], ACT.Copy, scale=1.0 / 16)
+        nc.scalar.activation(ns16[:], steep_sb[:], ACT.Copy, scale=-1.0 / 16)
+
+        soft = wide("soft")
+        soft_sum = small("soft_sum", 1)
+        shift = small("shift", 1)
+        e = wide("e")
+        nc.scalar.activation(soft[:], a[:], ACT.Exp, scale=1.0 / TEMPER, accum_out=soft_sum[:])
+        nc.scalar.activation(shift[:], soft_sum[:].bitcast(U32), ACT.Copy,
+                             scale=-TEMPER * math.log(2.0) / 2.0**23, bias=TEMPER * math.log(2.0) * 127)
+        sums = small("sums", 2 * G)
+        nc.vector.tensor_reduce(sums[:, 0:G], by_group(a[:]), AX.X, ALU.add)
+        nc.scalar.activation(e[:], a[:], ACT.Exp, bias=shift[:])
+        nc.vector.tensor_reduce(sums[:, G : 2 * G], by_group(ta[:]), AX.X, ALU.add)
+        blocks = sb.tile([P, 2 * B], F32, name="blocks", tag="held", align_bytes=64)
+        nc.vector.tensor_reduce(blocks[:], by_group(sums[:]), AX.X, ALU.add)
+        diff = small("diff", 2 * G)
+        nc.vector.scalar_tensor_tensor(by_group(diff[:]), spread(blocks[:], 8), -1.0 / 8, by_group(sums[:]), ALU.mult, ALU.add)
+        vg_bytes = sb.tile([P, I], U8, name="vg_bytes", tag="held", align_bytes=64)
+        h = I // 2
+        nc.vector.tensor_copy(vg_bytes[:, 0:h], v_bytes[:].indirect(offsets[:, 0 : h // 16]))
+        th = small("th")
+        nc.scalar.activation(th[:], diff[:, 0:G], ACT.Tanh, scale=s16[:])
+        gms = small("gms")
+        nc.scalar.activation(gms[:], th[:], ACT.Identity, scale=ns16[:], bias=s16[:])
+        gs8 = small("gs8")
+        nc.scalar.activation(gs8[:], th[:], ACT.Identity, scale=s16[:], bias=s16[:])
+
+        p = wide("p")
+        z = small("z", 1)
+        nc.vector.scalar_tensor_tensor(by_group(p[:]), spread(th[:], R), 1.0, by_group(e[:]), ALU.add, ALU.mult, accum_out=z[:])
+        nc.vector.tensor_copy(vg_bytes[:, h:I], v_bytes[:].indirect(offsets[:, h // 16 : I // 16]))
+        nc.tensor.matmul_mx(c0[:], lhsT=g_codes[:].bitcast(FP8X4), lhsT_scale=g_scales[:],
+                            rhs=vg_words[:].bitcast(FP4X4), rhs_scale=vg_bytes[:], start=True, stop=True)
+        rz = small("rz", 1)
+        nc.vector.reciprocal(rz[:], z[:])
+        gp = small("gp")
+        nc.vector.tensor_reduce(gp[:], by_group(p[:]), AX.X, ALU.add)
+        ks = small("ks")
+        nc.vector.scalar_tensor_tensor(ks[:], diff[:, G : 2 * G], rz[:], gms[:], ALU.mult, ALU.mult)
+        b2 = small("b2")
+        nc.vector.tensor_tensor(b2[:], gp[:], gms[:], ALU.mult)
+        y = wide("y")
+        ysum = small("ysum", 1)
+        nc.vector.scalar_tensor_tensor(y[:], c0[:], 512.0, p[:], ALU.mult, ALU.mult, accum_out=ysum[:])
+        cbar = small("cbar", 1)
+        nc.scalar.activation(cbar[:], ysum[:], ACT.Copy, scale=rz[:])
+        v = wide("v")
+        nc.vector.scalar_tensor_tensor(by_group(v[:]), by_group(ta[:]), rz[:], spread(ks[:], R), ALU.mult, ALU.add)
+        pc = wide("pc")
+        nc.vector.scalar_tensor_tensor(pc[:], p[:], cbar[:], y[:], ALU.mult, ALU.subtract)
+        w = wide("w")
+        tau = small("tau", 1)
+        nc.vector.scalar_tensor_tensor(w[:], p[:], 1.0, v[:], ALU.mult, ALU.mult, accum_out=tau[:])
+        taur = small("taur", 1)
+        nc.scalar.activation(taur[:], tau[:], ACT.Copy, scale=rz[:])
+        gpc = small("gpc")
+        nc.vector.tensor_reduce(gpc[:], by_group(pc[:]), AX.X, ALU.add)
+        gn = wide("gn")
+        nu = small("nu", 1)
+        nc.vector.scalar_tensor_tensor(gn[:], v[:], taur[:], pc[:], ALU.subtract, ALU.mult, accum_out=nu[:])
+        nur = small("nur", 1)
+        nc.scalar.activation(nur[:], nu[:], ACT.Copy, scale=rz[:])
+        gks = small("gks")
+        nc.vector.tensor_tensor(gks[:], gs8[:], ks[:], ALU.mult)
+        gg = small("gg")
+        nc.vector.tensor_reduce(gg[:], by_group(gn[:]), AX.X, ALU.add)
+        b1 = small("b1")
+        nc.vector.tensor_tensor(b1[:], gpc[:], gks[:], ALU.mult)
+        t1 = small("t1")
+        nc.vector.tensor_tensor(t1[:], gg[:], gms[:], ALU.mult)
+        b3 = small("b3")
+        nc.vector.scalar_tensor_tensor(b3[:], b2[:], nur[:], b1[:], ALU.mult, ALU.add)
+        f = wide("f")
+
+        def f_piece(lo, hi):
+            nc.vector.scalar_tensor_tensor(f[:, lo:hi], p[:, lo:hi], nur[:], gn[:, lo:hi], ALU.mult, ALU.subtract)
+
+        f_piece(0, 128)
+        x = small("x")
+        nc.vector.tensor_tensor(x[:], b3[:], t1[:], ALU.subtract)
+        f_piece(128, 320)
+        xb = small("xb", B)
+        nc.vector.tensor_reduce(xb[:], by_group(x[:]), AX.X, ALU.add)
+        f_piece(320, 512)
+        rg = small("rg")
+        nc.vector.scalar_tensor_tensor(by_group(rg[:]), spread(xb[:], 8), -1.0 / 8, by_group(x[:]), ALU.mult, ALU.add)
+        rx = wide("rx")
+        nc.vector.tensor_copy(by_group(rx[:]), spread(rg[:], R))
+        nc.vector.tensor_tensor(window[:].indirect(offsets[:]), f[:], rx[:], ALU.add)
+        edges = (0, 256, 768, 1280, 1792, 2048)
+        for c in range(len(edges) - 1):
+            cols = slice(edges[c], edges[c + 1])
+            res = sb.tile([P, edges[c + 1] - edges[c]], F32, name="res%d" % c)
+            nc.vector.tensor_tensor(res[:], window[:, cols], base_sb[:, cols], ALU.add)
+            nc.sync.dma_start(out[:, cols], res[:])

@@ -46,90 +46,105 @@ def tile_attend_hvblockcontrast_s_kernel(tc, query, keys_words, keys_scales, ste
         nc.sync.dma_start(offsets[:], offs)
 
         k_words = sb.tile([P, T], U16, name="k_words")
-        v_words = sb.tile([P, T], U16, name="v_words")
         k_bytes = sb.tile([P, T], U8, name="k_bytes")
         v_bytes = sb.tile([P, T], U8, name="v_bytes")
         window = sb.tile([P, T], F32, name="window")
-        nc.vector.memset(k_bytes[:].bitcast(I32), 0)
         nc.vector.memset(v_bytes[:].bitcast(I32), 0)
-        nc.vector.memset(window[:], 0.0)
-        warm = small("warm", 8)
-        nc.gpsimd.memset(warm[:], 0.0)
-        warm_out = small("warm_out", 8)
-        nc.scalar.activation(warm_out[:], warm[:], ACT.Exp)
+        warm = sb.tile([P, 8], F32, name="warm", tag="after_warm")
+        nc.vector.memset(warm[:], 0.0)
+        nc.gpsimd.memset(window[:], 0.0)
 
-        def load_bytes(tile, src):
+        def load_bytes(queue, tile, src):
             for quad in range(4):
-                nc.sync.dma_start(tile[32 * quad : 32 * quad + 4, :].bitcast(I32), src[0][4 * quad : 4 * quad + 4, :].bitcast(I32))
+                queue.dma_start(tile[32 * quad : 32 * quad + 4, :].bitcast(I32), src[0][4 * quad : 4 * quad + 4, :].bitcast(I32))
 
-        def load_rows(name, src):
-            raw = sb.tile([P, PACK, Q], F32, name=name)
+        def interleave(rows_bf, raw):
+            nc.scalar.copy(rows_bf[:].rearrange("p (c i) j -> p c j i", i=4), raw[:].rearrange("p j (c i) -> p c j i", i=4))
+
+        def load_rows(name, src, tag):
+            raw = sb.tile([P, PACK, Q], F32, name=name, tag=tag)
             nc.sync.dma_start(raw[:], src.rearrange("(p j) w -> p j w", j=PACK))
             return raw
 
+        for quad in range(4):
+            rows = keys_scales[0][4 * quad : 4 * quad + 4, :].bitcast(I32)
+            nc.sync.dma_start(k_bytes[32 * quad : 32 * quad + 32, :].bitcast(I32), rows.unsqueeze(0).to_broadcast([8, 4, T // 4]))
         nc.sync.dma_start(k_words[:].bitcast(I32), keys_words[0].bitcast(I32))
-        load_bytes(k_bytes, keys_scales)
-        q_raw = load_rows("q_raw", query)
-        dq_raw = load_rows("dq_raw", dquery)
+        q_raw = load_rows("q_raw", query, "after_q_raw")
+        dq_raw = load_rows("dq_raw", dquery, "dq_raw")
+        warm_out = sb.tile([P, 8], F32, name="warm_out", tag="after_warm_out")
+        nc.scalar.activation(warm_out[:], warm[:], ACT.Exp)
+        load_bytes(nc.sync, v_bytes, vals_scales)
+        v_words = sb.tile([P, T], U16, name="v_words", tag="after_warm")
         nc.sync.dma_start(v_words[:].bitcast(I32), vals_words[0].bitcast(I32))
-        load_bytes(v_bytes, vals_scales)
-        g_raw = load_rows("g_raw", gout)
+        g_raw = load_rows("g_raw", gout, "after_warm_out")
         steep_sb = small("steep_sb", 1)
         nc.sync.dma_start(steep_sb[:], steep)
-        cw = T // OUT_CHUNKS
-        base_sb = sb.tile([P, T], F32, name="base_sb")
-        nc.sync.dma_start(base_sb[:], base)
 
-        qq_bf = sb.tile([P, 2, Q, PACK], BF16, name="qq_bf", align_bytes=64)
-        g_bf = sb.tile([P, Q, PACK], BF16, name="g_bf", align_bytes=64)
-        nc.scalar.copy(qq_bf[:, 0], q_raw[:].rearrange("p j w -> p w j"))
-        nc.scalar.copy(qq_bf[:, 1], dq_raw[:].rearrange("p j w -> p w j"))
-        nc.scalar.copy(g_bf[:], g_raw[:].rearrange("p j w -> p w j"))
+        q_bf = sb.tile([P, Q, PACK], BF16, name="q_bf", tag="after_q", align_bytes=64)
+        dq_bf = sb.tile([P, Q, PACK], BF16, name="dq_bf", align_bytes=64)
+        interleave(q_bf, q_raw)
+        interleave(dq_bf, dq_raw)
+
+        base_sb = sb.tile([P, T], F32, name="base_sb", tag="after_q_raw")
+        nc.sync.dma_start(base_sb[:], base)
 
         kg_words = sb.tile([P, I], U16, name="kg_words", align_bytes=64)
         kg_bytes = sb.tile([P, I], U8, name="kg_bytes", align_bytes=64)
-        vg_words = sb.tile([P, I], U16, name="vg_words", align_bytes=64)
         qq_codes = sb.tile([P, 2 * Q], U32, name="qq_codes", align_bytes=64)
         qq_scales = sb.tile([P, 2 * Q], U8, name="qq_scales", align_bytes=64)
         g_codes = sb.tile([P, Q], U32, name="g_codes", align_bytes=64)
         g_scales = sb.tile([P, Q], U8, name="g_scales", align_bytes=64)
 
-        nc.vector.tensor_copy(kg_words[:], k_words[:].indirect(offsets[:]))
         nc.vector.tensor_copy(kg_bytes[:], k_bytes[:].indirect(offsets[:]))
+        nc.vector.tensor_copy(kg_words[:], k_words[:].indirect(offsets[:]))
         a = ps.tile([P, I], F32, name="a")
         ta = ps.tile([P, I], F32, name="ta")
         c0 = ps.tile([P, I], F32, name="c0")
-        for s, dst in enumerate((a, ta)):
+        h = I // 2
+        halves = ((slice(0, h), slice(0, h // 16)), (slice(h, I), slice(h // 16, I // 16)))
+
+        def scores(s, dst, rows_bf):
             cols = slice(s * Q, (s + 1) * Q)
-            nc.vector.quantize_mx(qq_codes[:, cols].bitcast(FP8X4), qq_scales[:, cols], qq_bf[:, s].rearrange("p w j -> p (w j)"))
+            nc.vector.quantize_mx(qq_codes[:, cols].bitcast(FP8X4), qq_scales[:, cols], rows_bf[:].rearrange("p w j -> p (w j)"))
             nc.tensor.matmul_mx(dst[:], lhsT=qq_codes[:, cols].bitcast(FP8X4), lhsT_scale=qq_scales[:, cols],
                                 rhs=kg_words[:].bitcast(FP4X4), rhs_scale=kg_bytes[:], start=True, stop=True)
-        nc.vector.tensor_copy(vg_words[:], v_words[:].indirect(offsets[:]))
-        nc.vector.quantize_mx(g_codes[:].bitcast(FP8X4), g_scales[:], g_bf[:].rearrange("p w j -> p (w j)"))
+
+        def gather_half(dst, src, half):
+            slots, entries = halves[half]
+            nc.vector.tensor_copy(dst[:, slots], src[:].indirect(offsets[:, entries]))
+
+        scores(0, a, q_bf)
+        vg_bytes = sb.tile([P, I], U8, name="vg_bytes", tag="after_q", align_bytes=64)
+        gather_half(vg_bytes, v_bytes, 0)
+        scores(1, ta, dq_bf)
+        gather_half(vg_bytes, v_bytes, 1)
 
         s16 = small("s16", 1)
         ns16 = small("ns16", 1)
         nc.scalar.activation(s16[:], steep_sb[:], ACT.Copy, scale=1.0 / 16)
         nc.scalar.activation(ns16[:], steep_sb[:], ACT.Copy, scale=-1.0 / 16)
 
-        soft = wide("soft")
+        soft = sb.tile([P, I], F32, name="soft", tag="after_soft", align_bytes=64)
         soft_sum = small("soft_sum", 1)
         shift = small("shift", 1)
         e = wide("e")
         nc.scalar.activation(soft[:], a[:], ACT.Exp, scale=1.0 / TEMPER, accum_out=soft_sum[:])
         nc.scalar.activation(shift[:], soft_sum[:].bitcast(U32), ACT.Copy,
                              scale=-TEMPER * math.log(2.0) / 2.0**23, bias=TEMPER * math.log(2.0) * 127)
+        g_bf = sb.tile([P, Q, PACK], BF16, name="g_bf", tag="after_soft", align_bytes=64)
+        interleave(g_bf, g_raw)
         sums = small("sums", 2 * G)
+        nc.vector.tensor_reduce(sums[:, G : 2 * G], by_group(ta[:]), AX.X, ALU.add)
         nc.vector.tensor_reduce(sums[:, 0:G], by_group(a[:]), AX.X, ALU.add)
         nc.scalar.activation(e[:], a[:], ACT.Exp, bias=shift[:])
-        nc.vector.tensor_reduce(sums[:, G : 2 * G], by_group(ta[:]), AX.X, ALU.add)
+        nc.vector.quantize_mx(g_codes[:].bitcast(FP8X4), g_scales[:], g_bf[:].rearrange("p w j -> p (w j)"))
         blocks = sb.tile([P, 2 * B], F32, name="blocks", tag="held", align_bytes=64)
         nc.vector.tensor_reduce(blocks[:], by_group(sums[:]), AX.X, ALU.add)
         diff = small("diff", 2 * G)
         nc.vector.scalar_tensor_tensor(by_group(diff[:]), spread(blocks[:], 8), -1.0 / 8, by_group(sums[:]), ALU.mult, ALU.add)
-        vg_bytes = sb.tile([P, I], U8, name="vg_bytes", tag="held", align_bytes=64)
-        h = I // 2
-        nc.vector.tensor_copy(vg_bytes[:, 0:h], v_bytes[:].indirect(offsets[:, 0 : h // 16]))
+        vg_words = sb.tile([P, I], U16, name="vg_words", tag="held", align_bytes=64)
+        gather_half(vg_words, v_words, 0)
         th = small("th")
         nc.scalar.activation(th[:], diff[:, 0:G], ACT.Tanh, scale=s16[:])
         gms = small("gms")
@@ -140,7 +155,7 @@ def tile_attend_hvblockcontrast_s_kernel(tc, query, keys_words, keys_scales, ste
         p = wide("p")
         z = small("z", 1)
         nc.vector.scalar_tensor_tensor(by_group(p[:]), spread(th[:], R), 1.0, by_group(e[:]), ALU.add, ALU.mult, accum_out=z[:])
-        nc.vector.tensor_copy(vg_bytes[:, h:I], v_bytes[:].indirect(offsets[:, h // 16 : I // 16]))
+        gather_half(vg_words, v_words, 1)
         nc.tensor.matmul_mx(c0[:], lhsT=g_codes[:].bitcast(FP8X4), lhsT_scale=g_scales[:],
                             rhs=vg_words[:].bitcast(FP4X4), rhs_scale=vg_bytes[:], start=True, stop=True)
         rz = small("rz", 1)

@@ -47,9 +47,9 @@ def tile_attend_hvblockcontrast_s_kernel(tc, query, keys_words, keys_scales, ste
 
         k_words = sb.tile([P, T], U16, name="k_words")
         k_bytes = sb.tile([P, T], U8, name="k_bytes")
-        v_bytes = sb.tile([P, T], U8, name="v_bytes")
         window = sb.tile([P, T], F32, name="window")
-        nc.vector.memset(v_bytes[:].bitcast(I32), 0)
+        nc.vector.memset(k_bytes[:, 0 : T // 2].bitcast(I32), 0)
+        nc.gpsimd.memset(k_bytes[:, T // 2 : T].bitcast(I32), 0)
         warm = sb.tile([P, 8], F32, name="warm", tag="after_warm")
         nc.vector.memset(warm[:], 0.0)
         nc.gpsimd.memset(window[:], 0.0)
@@ -66,27 +66,33 @@ def tile_attend_hvblockcontrast_s_kernel(tc, query, keys_words, keys_scales, ste
             nc.sync.dma_start(raw[:], src.rearrange("(p j) w -> p j w", j=PACK))
             return raw
 
-        for quad in range(4):
-            rows = keys_scales[0][4 * quad : 4 * quad + 4, :].bitcast(I32)
-            nc.sync.dma_start(k_bytes[32 * quad : 32 * quad + 32, :].bitcast(I32), rows.unsqueeze(0).to_broadcast([8, 4, T // 4]))
         nc.sync.dma_start(k_words[:].bitcast(I32), keys_words[0].bitcast(I32))
+        load_bytes(nc.sync, k_bytes, keys_scales)
         q_raw = load_rows("q_raw", query, "after_q_raw")
         dq_raw = load_rows("dq_raw", dquery, "dq_raw")
         warm_out = sb.tile([P, 8], F32, name="warm_out", tag="after_warm_out")
         nc.scalar.activation(warm_out[:], warm[:], ACT.Exp)
-        load_bytes(nc.sync, v_bytes, vals_scales)
         v_words = sb.tile([P, T], U16, name="v_words", tag="after_warm")
         nc.sync.dma_start(v_words[:].bitcast(I32), vals_words[0].bitcast(I32))
         g_raw = load_rows("g_raw", gout, "after_warm_out")
-        steep_sb = small("steep_sb", 1)
-        nc.sync.dma_start(steep_sb[:], steep)
+        v_bytes = sb.tile([P, T], U8, name="v_bytes")
+        nc.gpsimd.memset(v_bytes[:].bitcast(I32), 0)
+        load_bytes(nc.sync, v_bytes, vals_scales)
 
-        q_bf = sb.tile([P, Q, PACK], BF16, name="q_bf", tag="after_q", align_bytes=64)
-        dq_bf = sb.tile([P, Q, PACK], BF16, name="dq_bf", align_bytes=64)
+        q_bf = sb.tile([P, Q, PACK], BF16, name="q_bf", align_bytes=64)
+        dq_bf = sb.tile([P, Q, PACK], BF16, name="dq_bf", tag="after_dq", align_bytes=64)
         interleave(q_bf, q_raw)
         interleave(dq_bf, dq_raw)
+        g_bf = sb.tile([P, Q, PACK], BF16, name="g_bf", align_bytes=64)
+        interleave(g_bf, g_raw)
 
-        base_sb = sb.tile([P, T], F32, name="base_sb", tag="after_q_raw")
+        steep_sb = sb.tile([P, 1], F32, name="steep_sb", tag="after_q_raw")
+        nc.sync.dma_start(steep_sb[:], steep)
+        s16 = small("s16", 1)
+        ns16 = small("ns16", 1)
+        nc.scalar.activation(s16[:], steep_sb[:], ACT.Copy, scale=1.0 / 16)
+        nc.scalar.activation(ns16[:], steep_sb[:], ACT.Copy, scale=-1.0 / 16)
+        base_sb = sb.tile([P, T], F32, name="base_sb", tag="dq_raw")
         nc.sync.dma_start(base_sb[:], base)
 
         kg_words = sb.tile([P, I], U16, name="kg_words", align_bytes=64)
@@ -96,8 +102,8 @@ def tile_attend_hvblockcontrast_s_kernel(tc, query, keys_words, keys_scales, ste
         g_codes = sb.tile([P, Q], U32, name="g_codes", align_bytes=64)
         g_scales = sb.tile([P, Q], U8, name="g_scales", align_bytes=64)
 
-        nc.vector.tensor_copy(kg_bytes[:], k_bytes[:].indirect(offsets[:]))
         nc.vector.tensor_copy(kg_words[:], k_words[:].indirect(offsets[:]))
+        nc.vector.tensor_copy(kg_bytes[:], k_bytes[:].indirect(offsets[:]))
         a = ps.tile([P, I], F32, name="a")
         ta = ps.tile([P, I], F32, name="ta")
         c0 = ps.tile([P, I], F32, name="c0")
@@ -112,67 +118,59 @@ def tile_attend_hvblockcontrast_s_kernel(tc, query, keys_words, keys_scales, ste
 
         def gather_half(dst, src, half):
             slots, entries = halves[half]
-            nc.vector.tensor_copy(dst[:, slots], src[:].indirect(offsets[:, entries]))
+            nc.vector.tensor_copy(dst[:], src[:].indirect(offsets[:, entries]))
+            nc.tensor.matmul_mx(c0[:, slots], lhsT=g_codes[:].bitcast(FP8X4), lhsT_scale=g_scales[:],
+                                rhs=vg_words[:, slots].bitcast(FP4X4), rhs_scale=dst[:], start=True, stop=True)
 
         scores(0, a, q_bf)
-        vg_bytes = sb.tile([P, I], U8, name="vg_bytes", tag="after_q", align_bytes=64)
-        gather_half(vg_bytes, v_bytes, 0)
         scores(1, ta, dq_bf)
-        gather_half(vg_bytes, v_bytes, 1)
+        vg_words = sb.tile([P, I], U16, name="vg_words", tag="after_dq", align_bytes=64)
+        nc.vector.tensor_copy(vg_words[:], v_words[:].indirect(offsets[:]))
+        nc.vector.quantize_mx(g_codes[:].bitcast(FP8X4), g_scales[:], g_bf[:].rearrange("p w j -> p (w j)"))
 
-        s16 = small("s16", 1)
-        ns16 = small("ns16", 1)
-        nc.scalar.activation(s16[:], steep_sb[:], ACT.Copy, scale=1.0 / 16)
-        nc.scalar.activation(ns16[:], steep_sb[:], ACT.Copy, scale=-1.0 / 16)
 
-        soft = sb.tile([P, I], F32, name="soft", tag="after_soft", align_bytes=64)
+        soft = wide("soft")
         soft_sum = small("soft_sum", 1)
         shift = small("shift", 1)
-        e = wide("e")
+        e = sb.tile([P, I], F32, name="e", tag="after_e", align_bytes=64)
         nc.scalar.activation(soft[:], a[:], ACT.Exp, scale=1.0 / TEMPER, accum_out=soft_sum[:])
         nc.scalar.activation(shift[:], soft_sum[:].bitcast(U32), ACT.Copy,
                              scale=-TEMPER * math.log(2.0) / 2.0**23, bias=TEMPER * math.log(2.0) * 127)
-        g_bf = sb.tile([P, Q, PACK], BF16, name="g_bf", tag="after_soft", align_bytes=64)
-        interleave(g_bf, g_raw)
         sums = small("sums", 2 * G)
-        nc.vector.tensor_reduce(sums[:, G : 2 * G], by_group(ta[:]), AX.X, ALU.add)
         nc.vector.tensor_reduce(sums[:, 0:G], by_group(a[:]), AX.X, ALU.add)
         nc.scalar.activation(e[:], a[:], ACT.Exp, bias=shift[:])
-        nc.vector.quantize_mx(g_codes[:].bitcast(FP8X4), g_scales[:], g_bf[:].rearrange("p w j -> p (w j)"))
+        nc.vector.tensor_reduce(sums[:, G : 2 * G], by_group(ta[:]), AX.X, ALU.add)
         blocks = sb.tile([P, 2 * B], F32, name="blocks", tag="held", align_bytes=64)
         nc.vector.tensor_reduce(blocks[:], by_group(sums[:]), AX.X, ALU.add)
         diff = small("diff", 2 * G)
         nc.vector.scalar_tensor_tensor(by_group(diff[:]), spread(blocks[:], 8), -1.0 / 8, by_group(sums[:]), ALU.mult, ALU.add)
-        vg_words = sb.tile([P, I], U16, name="vg_words", tag="held", align_bytes=64)
-        gather_half(vg_words, v_words, 0)
+        vg_lo = sb.tile([P, h], U8, name="vg_lo", tag="held", align_bytes=64)
+        gather_half(vg_lo, v_bytes, 0)
         th = small("th")
         nc.scalar.activation(th[:], diff[:, 0:G], ACT.Tanh, scale=s16[:])
-        gms = small("gms")
-        nc.scalar.activation(gms[:], th[:], ACT.Identity, scale=ns16[:], bias=s16[:])
-        gs8 = small("gs8")
-        nc.scalar.activation(gs8[:], th[:], ACT.Identity, scale=s16[:], bias=s16[:])
+        gates = small("gates", 2 * G)
+        gms = gates[:, 0:G]
+        nc.scalar.activation(gms, th[:], ACT.Identity, scale=ns16[:], bias=s16[:])
+        nc.scalar.activation(gates[:, G : 2 * G], th[:], ACT.Identity, scale=s16[:], bias=s16[:])
 
         p = wide("p")
         z = small("z", 1)
         nc.vector.scalar_tensor_tensor(by_group(p[:]), spread(th[:], R), 1.0, by_group(e[:]), ALU.add, ALU.mult, accum_out=z[:])
-        gather_half(vg_words, v_words, 1)
-        nc.tensor.matmul_mx(c0[:], lhsT=g_codes[:].bitcast(FP8X4), lhsT_scale=g_scales[:],
-                            rhs=vg_words[:].bitcast(FP4X4), rhs_scale=vg_bytes[:], start=True, stop=True)
+        vg_hi = sb.tile([P, h], U8, name="vg_hi", tag="after_e", align_bytes=64)
+        gather_half(vg_hi, v_bytes, 1)
         rz = small("rz", 1)
         nc.vector.reciprocal(rz[:], z[:])
-        gp = small("gp")
-        nc.vector.tensor_reduce(gp[:], by_group(p[:]), AX.X, ALU.add)
-        ks = small("ks")
-        nc.vector.scalar_tensor_tensor(ks[:], diff[:, G : 2 * G], rz[:], gms[:], ALU.mult, ALU.mult)
-        b2 = small("b2")
-        nc.vector.tensor_tensor(b2[:], gp[:], gms[:], ALU.mult)
+        gpks = small("gpks", 2 * G)
+        ks = gpks[:, G : 2 * G]
+        nc.vector.tensor_reduce(gpks[:, 0:G], by_group(p[:]), AX.X, ALU.add)
+        nc.vector.scalar_tensor_tensor(ks, diff[:, G : 2 * G], rz[:], gms, ALU.mult, ALU.mult)
         y = wide("y")
         ysum = small("ysum", 1)
         nc.vector.scalar_tensor_tensor(y[:], c0[:], 512.0, p[:], ALU.mult, ALU.mult, accum_out=ysum[:])
         cbar = small("cbar", 1)
         nc.scalar.activation(cbar[:], ysum[:], ACT.Copy, scale=rz[:])
         v = wide("v")
-        nc.vector.scalar_tensor_tensor(by_group(v[:]), by_group(ta[:]), rz[:], spread(ks[:], R), ALU.mult, ALU.add)
+        nc.vector.scalar_tensor_tensor(by_group(v[:]), by_group(ta[:]), rz[:], spread(ks, R), ALU.mult, ALU.add)
         pc = wide("pc")
         nc.vector.scalar_tensor_tensor(pc[:], p[:], cbar[:], y[:], ALU.mult, ALU.subtract)
         w = wide("w")
@@ -187,16 +185,16 @@ def tile_attend_hvblockcontrast_s_kernel(tc, query, keys_words, keys_scales, ste
         nc.vector.scalar_tensor_tensor(gn[:], v[:], taur[:], pc[:], ALU.subtract, ALU.mult, accum_out=nu[:])
         nur = small("nur", 1)
         nc.scalar.activation(nur[:], nu[:], ACT.Copy, scale=rz[:])
-        gks = small("gks")
-        nc.vector.tensor_tensor(gks[:], gs8[:], ks[:], ALU.mult)
+        bk = small("bk", 2 * G)
+        nc.vector.tensor_tensor(bk[:], gpks[:], gates[:], ALU.mult)
         gg = small("gg")
         nc.vector.tensor_reduce(gg[:], by_group(gn[:]), AX.X, ALU.add)
         b1 = small("b1")
-        nc.vector.tensor_tensor(b1[:], gpc[:], gks[:], ALU.mult)
+        nc.vector.tensor_tensor(b1[:], gpc[:], bk[:, G : 2 * G], ALU.mult)
         t1 = small("t1")
-        nc.vector.tensor_tensor(t1[:], gg[:], gms[:], ALU.mult)
+        nc.vector.tensor_tensor(t1[:], gg[:], gms, ALU.mult)
         b3 = small("b3")
-        nc.vector.scalar_tensor_tensor(b3[:], b2[:], nur[:], b1[:], ALU.mult, ALU.add)
+        nc.vector.scalar_tensor_tensor(b3[:], bk[:, 0:G], nur[:], b1[:], ALU.mult, ALU.add)
         f = wide("f")
 
         def f_piece(lo, hi):
@@ -209,12 +207,10 @@ def tile_attend_hvblockcontrast_s_kernel(tc, query, keys_words, keys_scales, ste
         xb = small("xb", B)
         nc.vector.tensor_reduce(xb[:], by_group(x[:]), AX.X, ALU.add)
         f_piece(320, 512)
-        rg = small("rg")
-        nc.vector.scalar_tensor_tensor(by_group(rg[:]), spread(xb[:], 8), -1.0 / 8, by_group(x[:]), ALU.mult, ALU.add)
         rx = wide("rx")
-        nc.vector.tensor_copy(by_group(rx[:]), spread(rg[:], R))
+        nc.vector.scalar_tensor_tensor(by_group(rx[:]), spread(xb[:], I // B), -1.0 / 8, spread(x[:], R), ALU.mult, ALU.add)
         nc.vector.tensor_tensor(window[:].indirect(offsets[:]), f[:], rx[:], ALU.add)
-        edges = (0, 256, 768, 1280, 1792, 2048)
+        edges = (0, 128, 512, 1024, 1536, 1920, 2048)
         for c in range(len(edges) - 1):
             cols = slice(edges[c], edges[c + 1])
             res = sb.tile([P, edges[c + 1] - edges[c]], F32, name="res%d" % c)

@@ -16,203 +16,226 @@ ACT = mybir.ActivationFunctionType
 AX = mybir.AxisListType
 
 P = 128
-D, T, I, Q, G, B = 512, 2048, 512, 128, 64, 8
-R = I // G
+FEATURES = 512
+TOKENS = 2048
+SLOTS = 512
+ROWS = 128
+GROUPS = 64
+BLOCKS = 8
+FAN = 8
 PACK = 4
-TEMPER = 8.0
-OUT_CHUNKS = 4
-FLOPS = 3 * 2 * D * Q * I
+LIST_ROWS = 16
+GAIN = 512.0
+SOFTEN = 8.0
+F_EDGES = (0, 128, 320, 512)
+OUT_EDGES = (0, 256, 768, 1280, 1792, 2048)
+FLOPS = 3 * 2 * FEATURES * ROWS * SLOTS
 
 
-def tile_attend_hvblockcontrast_s_kernel(tc, query, keys_words, keys_scales, steep, gout, vals_words, vals_scales, dquery, base, offs, out):
+def tile_attend_hvblockcontrast_s_kernel(
+    tc, query, keys_words, keys_scales, steep, gout, vals_words, vals_scales, dquery, base, offs, out
+):
     nc = tc.nc
     with ExitStack() as ctx:
         sb = ctx.enter_context(tc.tile_pool(name="sb", bufs=1))
         ps = ctx.enter_context(tc.psum_pool(name="ps", bufs=1))
 
-        def small(name, n=G):
-            return sb.tile([P, n], F32, name=name)
+        def f32_tile(name, width):
+            return sb.tile([P, width], F32, name=name)
 
-        def wide(name):
-            return sb.tile([P, I], F32, name=name)
+        def in_eights(ap):
+            return ap.rearrange("p (g r) -> p g r", r=FAN)
 
-        def by_group(ap):
-            return ap.rearrange("p (g r) -> p g r", r=R)
+        def spread(ap, times):
+            return ap.unsqueeze(2).to_broadcast([P, ap.shape[1], times])
 
-        def spread(ap, n):
-            return ap.unsqueeze(2).to_broadcast([P, ap.shape[1], n])
-
-        offsets = sb.tile([P, I // 16], U16, name="offsets")
+        offsets = sb.tile([P, SLOTS // LIST_ROWS], U16, name="offsets")
         nc.sync.dma_start(offsets[:], offs)
 
-        k_words = sb.tile([P, T], U16, name="k_words")
-        k_bytes = sb.tile([P, T], U8, name="k_bytes")
-        window = sb.tile([P, T], F32, name="window")
-        nc.vector.memset(k_bytes[:, 0 : T // 2].bitcast(I32), 0)
-        nc.gpsimd.memset(k_bytes[:, T // 2 : T].bitcast(I32), 0)
-        warm = sb.tile([P, 8], F32, name="warm", tag="after_warm")
-        nc.vector.memset(warm[:], 0.0)
-        nc.gpsimd.memset(window[:], 0.0)
+        k_words = sb.tile([P, TOKENS], U16, name="k_words")
+        v_words = sb.tile([P, TOKENS], U16, name="v_words")
+        k_bytes = sb.tile([P, TOKENS], U8, name="k_bytes")
+        v_bytes = sb.tile([P, TOKENS], U8, name="v_bytes")
+        window = f32_tile("window", TOKENS)
+        nc.vector.memset(k_bytes[:].bitcast(I32), 0)
+        nc.vector.memset(v_bytes[:].bitcast(I32), 0)
+        nc.vector.memset(window[:], 0.0)
 
-        def load_bytes(queue, tile, src):
+        def load_scale_rows(tile, src):
             for quad in range(4):
-                queue.dma_start(tile[32 * quad : 32 * quad + 4, :].bitcast(I32), src[0][4 * quad : 4 * quad + 4, :].bitcast(I32))
+                rows = src[0][4 * quad : 4 * quad + 4, :]
+                nc.sync.dma_start(tile[32 * quad : 32 * quad + 4, :].bitcast(I32), rows.bitcast(I32))
 
-        def interleave(rows_bf, raw):
-            nc.scalar.copy(rows_bf[:].rearrange("p (c i) j -> p c j i", i=4), raw[:].rearrange("p j (c i) -> p c j i", i=4))
-
-        def load_rows(name, src, tag):
-            raw = sb.tile([P, PACK, Q], F32, name=name, tag=tag)
+        def load_operand(name, src):
+            raw = sb.tile([P, PACK, ROWS], F32, name=name)
             nc.sync.dma_start(raw[:], src.rearrange("(p j) w -> p j w", j=PACK))
             return raw
 
         nc.sync.dma_start(k_words[:].bitcast(I32), keys_words[0].bitcast(I32))
-        load_bytes(nc.sync, k_bytes, keys_scales)
-        q_raw = load_rows("q_raw", query, "after_q_raw")
-        dq_raw = load_rows("dq_raw", dquery, "dq_raw")
-        warm_out = sb.tile([P, 8], F32, name="warm_out", tag="after_warm_out")
-        nc.scalar.activation(warm_out[:], warm[:], ACT.Exp)
-        v_words = sb.tile([P, T], U16, name="v_words", tag="after_warm")
+        load_scale_rows(k_bytes, keys_scales)
+        q_raw = load_operand("q_raw", query)
+        dq_raw = load_operand("dq_raw", dquery)
         nc.sync.dma_start(v_words[:].bitcast(I32), vals_words[0].bitcast(I32))
-        g_raw = load_rows("g_raw", gout, "after_warm_out")
-        v_bytes = sb.tile([P, T], U8, name="v_bytes")
-        nc.gpsimd.memset(v_bytes[:].bitcast(I32), 0)
-        load_bytes(nc.sync, v_bytes, vals_scales)
-
-        q_bf = sb.tile([P, Q, PACK], BF16, name="q_bf", align_bytes=64)
-        dq_bf = sb.tile([P, Q, PACK], BF16, name="dq_bf", tag="after_dq", align_bytes=64)
-        interleave(q_bf, q_raw)
-        interleave(dq_bf, dq_raw)
-        g_bf = sb.tile([P, Q, PACK], BF16, name="g_bf", align_bytes=64)
-        interleave(g_bf, g_raw)
-
-        steep_sb = sb.tile([P, 1], F32, name="steep_sb", tag="after_q_raw")
+        gout_raw = load_operand("gout_raw", gout)
+        load_scale_rows(v_bytes, vals_scales)
+        steep_sb = f32_tile("steep_sb", 1)
         nc.sync.dma_start(steep_sb[:], steep)
-        s16 = small("s16", 1)
-        ns16 = small("ns16", 1)
-        nc.scalar.activation(s16[:], steep_sb[:], ACT.Copy, scale=1.0 / 16)
-        nc.scalar.activation(ns16[:], steep_sb[:], ACT.Copy, scale=-1.0 / 16)
-        base_sb = sb.tile([P, T], F32, name="base_sb", tag="dq_raw")
+        base_sb = f32_tile("base_sb", TOKENS)
         nc.sync.dma_start(base_sb[:], base)
 
-        kg_words = sb.tile([P, I], U16, name="kg_words", align_bytes=64)
-        kg_bytes = sb.tile([P, I], U8, name="kg_bytes", align_bytes=64)
-        qq_codes = sb.tile([P, 2 * Q], U32, name="qq_codes", align_bytes=64)
-        qq_scales = sb.tile([P, 2 * Q], U8, name="qq_scales", align_bytes=64)
-        g_codes = sb.tile([P, Q], U32, name="g_codes", align_bytes=64)
-        g_scales = sb.tile([P, Q], U8, name="g_scales", align_bytes=64)
+        q_bf = sb.tile([P, ROWS, PACK], BF16, name="q_bf", tag="behind_q", align_bytes=64)
+        dq_bf = sb.tile([P, ROWS, PACK], BF16, name="dq_bf", tag="behind_dq", align_bytes=64)
+        gout_bf = sb.tile([P, ROWS, PACK], BF16, name="gout_bf", align_bytes=64)
+        for rows_bf, raw in ((q_bf, q_raw), (dq_bf, dq_raw), (gout_bf, gout_raw)):
+            nc.scalar.copy(rows_bf[:], raw[:].rearrange("p j w -> p w j"))
+        steep16 = f32_tile("steep16", 1)
+        minus_steep16 = f32_tile("minus_steep16", 1)
+        nc.scalar.activation(steep16[:], steep_sb[:], ACT.Copy, scale=0.5 / FAN)
+        nc.scalar.activation(minus_steep16[:], steep_sb[:], ACT.Copy, scale=-0.5 / FAN)
 
-        nc.vector.tensor_copy(kg_words[:], k_words[:].indirect(offsets[:]))
-        nc.vector.tensor_copy(kg_bytes[:], k_bytes[:].indirect(offsets[:]))
-        a = ps.tile([P, I], F32, name="a")
-        ta = ps.tile([P, I], F32, name="ta")
-        c0 = ps.tile([P, I], F32, name="c0")
-        h = I // 2
-        halves = ((slice(0, h), slice(0, h // 16)), (slice(h, I), slice(h // 16, I // 16)))
+        k_words_listed = sb.tile([P, SLOTS], U16, name="k_words_listed", align_bytes=64)
+        k_bytes_listed = sb.tile([P, SLOTS], U8, name="k_bytes_listed", align_bytes=64)
+        q_codes = sb.tile([P, 2 * ROWS], U32, name="q_codes", align_bytes=64)
+        q_scales = sb.tile([P, 2 * ROWS], U8, name="q_scales", align_bytes=64)
+        gout_codes = sb.tile([P, ROWS], U32, name="gout_codes", align_bytes=64)
+        gout_scales = sb.tile([P, ROWS], U8, name="gout_scales", align_bytes=64)
 
-        def scores(s, dst, rows_bf):
-            cols = slice(s * Q, (s + 1) * Q)
-            nc.vector.quantize_mx(qq_codes[:, cols].bitcast(FP8X4), qq_scales[:, cols], rows_bf[:].rearrange("p w j -> p (w j)"))
-            nc.tensor.matmul_mx(dst[:], lhsT=qq_codes[:, cols].bitcast(FP8X4), lhsT_scale=qq_scales[:, cols],
-                                rhs=kg_words[:].bitcast(FP4X4), rhs_scale=kg_bytes[:], start=True, stop=True)
+        nc.vector.tensor_copy(k_words_listed[:], k_words[:].indirect(offsets[:]))
+        nc.vector.tensor_copy(k_bytes_listed[:], k_bytes[:].indirect(offsets[:]))
+        a = ps.tile([P, SLOTS], F32, name="a")
+        ta = ps.tile([P, SLOTS], F32, name="ta")
+        c0 = ps.tile([P, SLOTS], F32, name="c0")
+        half = SLOTS // 2
 
-        def gather_half(dst, src, half):
-            slots, entries = halves[half]
-            nc.vector.tensor_copy(dst[:], src[:].indirect(offsets[:, entries]))
-            nc.tensor.matmul_mx(c0[:, slots], lhsT=g_codes[:].bitcast(FP8X4), lhsT_scale=g_scales[:],
-                                rhs=vg_words[:, slots].bitcast(FP4X4), rhs_scale=dst[:], start=True, stop=True)
+        def scores(place, dst, rows_bf):
+            cols = slice(place * ROWS, (place + 1) * ROWS)
+            nc.vector.quantize_mx(
+                q_codes[:, cols].bitcast(FP8X4), q_scales[:, cols], rows_bf[:].rearrange("p w j -> p (w j)")
+            )
+            nc.tensor.matmul_mx(
+                dst[:], lhsT=q_codes[:, cols].bitcast(FP8X4), lhsT_scale=q_scales[:, cols],
+                rhs=k_words_listed[:].bitcast(FP4X4), rhs_scale=k_bytes_listed[:], start=True, stop=True,
+            )
+
+        def c0_half(first, bytes_listed):
+            entries = slice(first // LIST_ROWS, (first + half) // LIST_ROWS)
+            slots = slice(first, first + half)
+            nc.vector.tensor_copy(bytes_listed[:], v_bytes[:].indirect(offsets[:, entries]))
+            nc.tensor.matmul_mx(
+                c0[:, slots], lhsT=gout_codes[:].bitcast(FP8X4), lhsT_scale=gout_scales[:],
+                rhs=v_words_listed[:, slots].bitcast(FP4X4), rhs_scale=bytes_listed[:], start=True, stop=True,
+            )
 
         scores(0, a, q_bf)
         scores(1, ta, dq_bf)
-        vg_words = sb.tile([P, I], U16, name="vg_words", tag="after_dq", align_bytes=64)
-        nc.vector.tensor_copy(vg_words[:], v_words[:].indirect(offsets[:]))
-        nc.vector.quantize_mx(g_codes[:].bitcast(FP8X4), g_scales[:], g_bf[:].rearrange("p w j -> p (w j)"))
+        v_words_listed = sb.tile([P, SLOTS], U16, name="v_words_listed", tag="behind_dq", align_bytes=64)
+        nc.vector.tensor_copy(v_words_listed[:], v_words[:].indirect(offsets[:]))
+        nc.vector.quantize_mx(
+            gout_codes[:].bitcast(FP8X4), gout_scales[:], gout_bf[:].rearrange("p w j -> p (w j)")
+        )
+        v_bytes_low = sb.tile([P, half], U8, name="v_bytes_low", tag="behind_q", align_bytes=64)
+        c0_half(0, v_bytes_low)
 
+        soft = f32_tile("soft", SLOTS)
+        soft_sum = f32_tile("soft_sum", 1)
+        minus_shift = f32_tile("minus_shift", 1)
+        e = f32_tile("e", SLOTS)
+        nc.scalar.activation(soft[:], a[:], ACT.Exp, scale=1.0 / SOFTEN, accum_out=soft_sum[:])
+        nc.scalar.activation(
+            minus_shift[:], soft_sum[:].bitcast(U32), ACT.Copy,
+            scale=-SOFTEN * math.log(2.0) / 2.0**23,
+            bias=SOFTEN * math.log(2.0) * (127 + math.log2(SLOTS) / 2),
+        )
 
-        soft = wide("soft")
-        soft_sum = small("soft_sum", 1)
-        shift = small("shift", 1)
-        e = sb.tile([P, I], F32, name="e", tag="after_e", align_bytes=64)
-        nc.scalar.activation(soft[:], a[:], ACT.Exp, scale=1.0 / TEMPER, accum_out=soft_sum[:])
-        nc.scalar.activation(shift[:], soft_sum[:].bitcast(U32), ACT.Copy,
-                             scale=-TEMPER * math.log(2.0) / 2.0**23, bias=TEMPER * math.log(2.0) * 127)
-        sums = small("sums", 2 * G)
-        nc.vector.tensor_reduce(sums[:, 0:G], by_group(a[:]), AX.X, ALU.add)
-        nc.scalar.activation(e[:], a[:], ACT.Exp, bias=shift[:])
-        nc.vector.tensor_reduce(sums[:, G : 2 * G], by_group(ta[:]), AX.X, ALU.add)
-        blocks = sb.tile([P, 2 * B], F32, name="blocks", tag="held", align_bytes=64)
-        nc.vector.tensor_reduce(blocks[:], by_group(sums[:]), AX.X, ALU.add)
-        diff = small("diff", 2 * G)
-        nc.vector.scalar_tensor_tensor(by_group(diff[:]), spread(blocks[:], 8), -1.0 / 8, by_group(sums[:]), ALU.mult, ALU.add)
-        vg_lo = sb.tile([P, h], U8, name="vg_lo", tag="held", align_bytes=64)
-        gather_half(vg_lo, v_bytes, 0)
-        th = small("th")
-        nc.scalar.activation(th[:], diff[:, 0:G], ACT.Tanh, scale=s16[:])
-        gates = small("gates", 2 * G)
-        gms = gates[:, 0:G]
-        nc.scalar.activation(gms, th[:], ACT.Identity, scale=ns16[:], bias=s16[:])
-        nc.scalar.activation(gates[:, G : 2 * G], th[:], ACT.Identity, scale=s16[:], bias=s16[:])
+        sums = f32_tile("sums", 2 * GROUPS)
+        nc.vector.tensor_reduce(sums[:, 0:GROUPS], in_eights(a[:]), AX.X, ALU.add)
+        nc.scalar.activation(e[:], a[:], ACT.Exp, bias=minus_shift[:])
+        nc.vector.tensor_reduce(sums[:, GROUPS : 2 * GROUPS], in_eights(ta[:]), AX.X, ALU.add)
+        block_sums = sb.tile([P, 2 * BLOCKS], F32, name="block_sums", tag="behind_diff", align_bytes=64)
+        nc.vector.tensor_reduce(block_sums[:], in_eights(sums[:]), AX.X, ALU.add)
+        diff = f32_tile("diff", 2 * GROUPS)
+        nc.vector.scalar_tensor_tensor(
+            in_eights(diff[:]), spread(block_sums[:], FAN), -1.0 / FAN, in_eights(sums[:]), ALU.mult, ALU.add
+        )
+        v_bytes_high = sb.tile([P, half], U8, name="v_bytes_high", tag="behind_diff", align_bytes=64)
+        c0_half(half, v_bytes_high)
+        th = f32_tile("th", GROUPS)
+        nc.scalar.activation(th[:], diff[:, 0:GROUPS], ACT.Tanh, scale=steep16[:])
+        gates = f32_tile("gates", 2 * GROUPS)
+        shut = gates[:, 0:GROUPS]
+        nc.scalar.activation(shut, th[:], ACT.Identity, scale=minus_steep16[:], bias=steep16[:])
+        nc.scalar.activation(gates[:, GROUPS : 2 * GROUPS], th[:], ACT.Identity, scale=steep16[:], bias=steep16[:])
 
-        p = wide("p")
-        z = small("z", 1)
-        nc.vector.scalar_tensor_tensor(by_group(p[:]), spread(th[:], R), 1.0, by_group(e[:]), ALU.add, ALU.mult, accum_out=z[:])
-        vg_hi = sb.tile([P, h], U8, name="vg_hi", tag="after_e", align_bytes=64)
-        gather_half(vg_hi, v_bytes, 1)
-        rz = small("rz", 1)
+        p = f32_tile("p", SLOTS)
+        z = f32_tile("z", 1)
+        nc.vector.scalar_tensor_tensor(
+            in_eights(p[:]), spread(th[:], FAN), 1.0, in_eights(e[:]), ALU.add, ALU.mult, accum_out=z[:]
+        )
+        rz = f32_tile("rz", 1)
         nc.vector.reciprocal(rz[:], z[:])
-        gpks = small("gpks", 2 * G)
-        ks = gpks[:, G : 2 * G]
-        nc.vector.tensor_reduce(gpks[:, 0:G], by_group(p[:]), AX.X, ALU.add)
-        nc.vector.scalar_tensor_tensor(ks, diff[:, G : 2 * G], rz[:], gms, ALU.mult, ALU.mult)
-        y = wide("y")
-        ysum = small("ysum", 1)
-        nc.vector.scalar_tensor_tensor(y[:], c0[:], 512.0, p[:], ALU.mult, ALU.mult, accum_out=ysum[:])
-        cbar = small("cbar", 1)
-        nc.scalar.activation(cbar[:], ysum[:], ACT.Copy, scale=rz[:])
-        v = wide("v")
-        nc.vector.scalar_tensor_tensor(by_group(v[:]), by_group(ta[:]), rz[:], spread(ks, R), ALU.mult, ALU.add)
-        pc = wide("pc")
-        nc.vector.scalar_tensor_tensor(pc[:], p[:], cbar[:], y[:], ALU.mult, ALU.subtract)
-        w = wide("w")
-        tau = small("tau", 1)
-        nc.vector.scalar_tensor_tensor(w[:], p[:], 1.0, v[:], ALU.mult, ALU.mult, accum_out=tau[:])
-        taur = small("taur", 1)
-        nc.scalar.activation(taur[:], tau[:], ACT.Copy, scale=rz[:])
-        gpc = small("gpc")
-        nc.vector.tensor_reduce(gpc[:], by_group(pc[:]), AX.X, ALU.add)
-        gn = wide("gn")
-        nu = small("nu", 1)
-        nc.vector.scalar_tensor_tensor(gn[:], v[:], taur[:], pc[:], ALU.subtract, ALU.mult, accum_out=nu[:])
-        nur = small("nur", 1)
-        nc.scalar.activation(nur[:], nu[:], ACT.Copy, scale=rz[:])
-        bk = small("bk", 2 * G)
-        nc.vector.tensor_tensor(bk[:], gpks[:], gates[:], ALU.mult)
-        gg = small("gg")
-        nc.vector.tensor_reduce(gg[:], by_group(gn[:]), AX.X, ALU.add)
-        b1 = small("b1")
-        nc.vector.tensor_tensor(b1[:], gpc[:], bk[:, G : 2 * G], ALU.mult)
-        t1 = small("t1")
-        nc.vector.tensor_tensor(t1[:], gg[:], gms, ALU.mult)
-        b3 = small("b3")
-        nc.vector.scalar_tensor_tensor(b3[:], bk[:, 0:G], nur[:], b1[:], ALU.mult, ALU.add)
-        f = wide("f")
+        p_sums_and_k = f32_tile("p_sums_and_k", 2 * GROUPS)
+        k_rz = p_sums_and_k[:, GROUPS : 2 * GROUPS]
+        nc.vector.tensor_reduce(p_sums_and_k[:, 0:GROUPS], in_eights(p[:]), AX.X, ALU.add)
+        nc.vector.scalar_tensor_tensor(k_rz, diff[:, GROUPS : 2 * GROUPS], rz[:], shut, ALU.mult, ALU.mult)
+        p_c0 = f32_tile("p_c0", SLOTS)
+        p_c0_sum = f32_tile("p_c0_sum", 1)
+        nc.vector.scalar_tensor_tensor(p_c0[:], c0[:], GAIN, p[:], ALU.mult, ALU.mult, accum_out=p_c0_sum[:])
+        c0_mean = f32_tile("c0_mean", 1)
+        nc.scalar.activation(c0_mean[:], p_c0_sum[:], ACT.Copy, scale=rz[:])
+        u_rz = f32_tile("u_rz", SLOTS)
+        nc.vector.scalar_tensor_tensor(
+            in_eights(u_rz[:]), in_eights(ta[:]), rz[:], spread(k_rz, FAN), ALU.mult, ALU.add
+        )
+        minus_pc = f32_tile("minus_pc", SLOTS)
+        nc.vector.scalar_tensor_tensor(minus_pc[:], p[:], c0_mean[:], p_c0[:], ALU.mult, ALU.subtract)
+        wu = f32_tile("wu", SLOTS)
+        tau = f32_tile("tau", 1)
+        nc.vector.scalar_tensor_tensor(wu[:], p[:], 1.0, u_rz[:], ALU.mult, ALU.mult, accum_out=tau[:])
+        tau_rz = f32_tile("tau_rz", 1)
+        nc.scalar.activation(tau_rz[:], tau[:], ACT.Copy, scale=rz[:])
+        minus_pc_sums = f32_tile("minus_pc_sums", GROUPS)
+        nc.vector.tensor_reduce(minus_pc_sums[:], in_eights(minus_pc[:]), AX.X, ALU.add)
+        minus_wcu = f32_tile("minus_wcu", SLOTS)
+        minus_nu = f32_tile("minus_nu", 1)
+        nc.vector.scalar_tensor_tensor(
+            minus_wcu[:], u_rz[:], tau_rz[:], minus_pc[:], ALU.subtract, ALU.mult, accum_out=minus_nu[:]
+        )
+        minus_nu_rz = f32_tile("minus_nu_rz", 1)
+        nc.scalar.activation(minus_nu_rz[:], minus_nu[:], ACT.Copy, scale=rz[:])
 
-        def f_piece(lo, hi):
-            nc.vector.scalar_tensor_tensor(f[:, lo:hi], p[:, lo:hi], nur[:], gn[:, lo:hi], ALU.mult, ALU.subtract)
+        gated = f32_tile("gated", 2 * GROUPS)
+        nc.vector.tensor_tensor(gated[:], p_sums_and_k[:], gates[:], ALU.mult)
+        minus_wcu_sums = f32_tile("minus_wcu_sums", GROUPS)
+        nc.vector.tensor_reduce(minus_wcu_sums[:], in_eights(minus_wcu[:]), AX.X, ALU.add)
+        x_wc = f32_tile("x_wc", GROUPS)
+        nc.vector.tensor_tensor(x_wc[:], minus_pc_sums[:], gated[:, GROUPS : 2 * GROUPS], ALU.mult)
+        minus_x_wcu = f32_tile("minus_x_wcu", GROUPS)
+        nc.vector.tensor_tensor(minus_x_wcu[:], minus_wcu_sums[:], shut, ALU.mult)
+        x_rest = f32_tile("x_rest", GROUPS)
+        nc.vector.scalar_tensor_tensor(x_rest[:], gated[:, 0:GROUPS], minus_nu_rz[:], x_wc[:], ALU.mult, ALU.add)
+        f = f32_tile("f", SLOTS)
 
-        f_piece(0, 128)
-        x = small("x")
-        nc.vector.tensor_tensor(x[:], b3[:], t1[:], ALU.subtract)
-        f_piece(128, 320)
-        xb = small("xb", B)
-        nc.vector.tensor_reduce(xb[:], by_group(x[:]), AX.X, ALU.add)
-        f_piece(320, 512)
-        rx = wide("rx")
-        nc.vector.scalar_tensor_tensor(by_group(rx[:]), spread(xb[:], I // B), -1.0 / 8, spread(x[:], R), ALU.mult, ALU.add)
-        nc.vector.tensor_tensor(window[:].indirect(offsets[:]), f[:], rx[:], ALU.add)
-        edges = (0, 128, 512, 1024, 1536, 1920, 2048)
-        for c in range(len(edges) - 1):
-            cols = slice(edges[c], edges[c + 1])
-            res = sb.tile([P, edges[c + 1] - edges[c]], F32, name="res%d" % c)
-            nc.vector.tensor_tensor(res[:], window[:, cols], base_sb[:, cols], ALU.add)
-            nc.sync.dma_start(out[:, cols], res[:])
+        def f_piece(piece):
+            slots = slice(F_EDGES[piece], F_EDGES[piece + 1])
+            nc.vector.scalar_tensor_tensor(
+                f[:, slots], p[:, slots], minus_nu_rz[:], minus_wcu[:, slots], ALU.mult, ALU.subtract
+            )
+
+        f_piece(0)
+        x = f32_tile("x", GROUPS)
+        nc.vector.tensor_tensor(x[:], x_rest[:], minus_x_wcu[:], ALU.subtract)
+        f_piece(1)
+        x_block_sums = f32_tile("x_block_sums", BLOCKS)
+        nc.vector.tensor_reduce(x_block_sums[:], in_eights(x[:]), AX.X, ALU.add)
+        f_piece(2)
+        r = f32_tile("r", SLOTS)
+        nc.vector.scalar_tensor_tensor(
+            in_eights(r[:]), spread(x_block_sums[:], FAN * FAN), -1.0 / FAN, spread(x[:], FAN), ALU.mult, ALU.add
+        )
+
+        nc.vector.tensor_tensor(window[:].indirect(offsets[:]), f[:], r[:], ALU.add)
+        for piece in range(len(OUT_EDGES) - 1):
+            cols = slice(OUT_EDGES[piece], OUT_EDGES[piece + 1])
+            result = f32_tile("result%d" % piece, OUT_EDGES[piece + 1] - OUT_EDGES[piece])
+            nc.vector.tensor_tensor(result[:], window[:, cols], base_sb[:, cols], ALU.add)
+            nc.sync.dma_start(out[:, cols], result[:])

import math
from contextlib import ExitStack

import concourse.mybir as mybir

F32 = mybir.dt.float32
BF16 = mybir.dt.bfloat16
I32 = mybir.dt.int32
U32 = mybir.dt.uint32
U16 = mybir.dt.uint16
U8 = mybir.dt.uint8
FP8X4 = mybir.dt.float8_e4m3fn_x4
FP4X4 = mybir.dt.float4_e2m1fn_x4
ALU = mybir.AluOpType
ACT = mybir.ActivationFunctionType
AX = mybir.AxisListType

P = 128
FEATURES = 512
TOKENS = 2048
SLOTS = 512
ROWS = 128
GROUPS = 64
BLOCKS = 8
FAN = 8
PACK = 4
LIST_ROWS = 16
GAIN = 512.0
SOFTEN = 8.0
F_EDGES = (0, 128, 320, 512)
OUT_EDGES = (0, 256, 768, 1280, 1792, 2048)
FLOPS = 3 * 2 * FEATURES * ROWS * SLOTS


def tile_attend_hvblockcontrast_s_kernel(
    tc, query, keys_words, keys_scales, steep, gout, vals_words, vals_scales, dquery, base, offs, out
):
    nc = tc.nc
    with ExitStack() as ctx:
        sb = ctx.enter_context(tc.tile_pool(name="sb", bufs=1))
        ps = ctx.enter_context(tc.psum_pool(name="ps", bufs=1))

        def f32_tile(name, width):
            return sb.tile([P, width], F32, name=name)

        def in_eights(ap):
            return ap.rearrange("p (g r) -> p g r", r=FAN)

        def spread(ap, times):
            return ap.unsqueeze(2).to_broadcast([P, ap.shape[1], times])

        offsets = sb.tile([P, SLOTS // LIST_ROWS], U16, name="offsets")
        nc.sync.dma_start(offsets[:], offs)

        k_words = sb.tile([P, TOKENS], U16, name="k_words")
        v_words = sb.tile([P, TOKENS], U16, name="v_words")
        k_bytes = sb.tile([P, TOKENS], U8, name="k_bytes")
        v_bytes = sb.tile([P, TOKENS], U8, name="v_bytes")
        window = f32_tile("window", TOKENS)
        nc.vector.memset(k_bytes[:].bitcast(I32), 0)
        nc.vector.memset(v_bytes[:].bitcast(I32), 0)
        nc.vector.memset(window[:], 0.0)

        def load_scale_rows(tile, src):
            for quad in range(4):
                rows = src[0][4 * quad : 4 * quad + 4, :]
                nc.sync.dma_start(tile[32 * quad : 32 * quad + 4, :].bitcast(I32), rows.bitcast(I32))

        def load_operand(name, src):
            raw = sb.tile([P, PACK, ROWS], F32, name=name)
            nc.sync.dma_start(raw[:], src.rearrange("(p j) w -> p j w", j=PACK))
            return raw

        nc.sync.dma_start(k_words[:].bitcast(I32), keys_words[0].bitcast(I32))
        load_scale_rows(k_bytes, keys_scales)
        q_raw = load_operand("q_raw", query)
        dq_raw = load_operand("dq_raw", dquery)
        nc.sync.dma_start(v_words[:].bitcast(I32), vals_words[0].bitcast(I32))
        gout_raw = load_operand("gout_raw", gout)
        load_scale_rows(v_bytes, vals_scales)
        steep_sb = f32_tile("steep_sb", 1)
        nc.sync.dma_start(steep_sb[:], steep)
        base_sb = f32_tile("base_sb", TOKENS)
        nc.sync.dma_start(base_sb[:], base)

        q_bf = sb.tile([P, ROWS, PACK], BF16, name="q_bf", tag="behind_q", align_bytes=64)
        dq_bf = sb.tile([P, ROWS, PACK], BF16, name="dq_bf", tag="behind_dq", align_bytes=64)
        gout_bf = sb.tile([P, ROWS, PACK], BF16, name="gout_bf", align_bytes=64)
        for rows_bf, raw in ((q_bf, q_raw), (dq_bf, dq_raw), (gout_bf, gout_raw)):
            nc.scalar.copy(rows_bf[:], raw[:].rearrange("p j w -> p w j"))
        steep16 = f32_tile("steep16", 1)
        minus_steep16 = f32_tile("minus_steep16", 1)
        nc.scalar.activation(steep16[:], steep_sb[:], ACT.Copy, scale=0.5 / FAN)
        nc.scalar.activation(minus_steep16[:], steep_sb[:], ACT.Copy, scale=-0.5 / FAN)

        k_words_listed = sb.tile([P, SLOTS], U16, name="k_words_listed", align_bytes=64)
        k_bytes_listed = sb.tile([P, SLOTS], U8, name="k_bytes_listed", align_bytes=64)
        q_codes = sb.tile([P, 2 * ROWS], U32, name="q_codes", align_bytes=64)
        q_scales = sb.tile([P, 2 * ROWS], U8, name="q_scales", align_bytes=64)
        gout_codes = sb.tile([P, ROWS], U32, name="gout_codes", align_bytes=64)
        gout_scales = sb.tile([P, ROWS], U8, name="gout_scales", align_bytes=64)

        nc.vector.tensor_copy(k_words_listed[:], k_words[:].indirect(offsets[:]))
        nc.vector.tensor_copy(k_bytes_listed[:], k_bytes[:].indirect(offsets[:]))
        a = ps.tile([P, SLOTS], F32, name="a")
        ta = ps.tile([P, SLOTS], F32, name="ta")
        c0 = ps.tile([P, SLOTS], F32, name="c0")
        half = SLOTS // 2

        def scores(place, dst, rows_bf):
            cols = slice(place * ROWS, (place + 1) * ROWS)
            nc.vector.quantize_mx(
                q_codes[:, cols].bitcast(FP8X4), q_scales[:, cols], rows_bf[:].rearrange("p w j -> p (w j)")
            )
            nc.tensor.matmul_mx(
                dst[:], lhsT=q_codes[:, cols].bitcast(FP8X4), lhsT_scale=q_scales[:, cols],
                rhs=k_words_listed[:].bitcast(FP4X4), rhs_scale=k_bytes_listed[:], start=True, stop=True,
            )

        def c0_half(first, bytes_listed):
            entries = slice(first // LIST_ROWS, (first + half) // LIST_ROWS)
            slots = slice(first, first + half)
            nc.vector.tensor_copy(bytes_listed[:], v_bytes[:].indirect(offsets[:, entries]))
            nc.tensor.matmul_mx(
                c0[:, slots], lhsT=gout_codes[:].bitcast(FP8X4), lhsT_scale=gout_scales[:],
                rhs=v_words_listed[:, slots].bitcast(FP4X4), rhs_scale=bytes_listed[:], start=True, stop=True,
            )

        scores(0, a, q_bf)
        scores(1, ta, dq_bf)
        v_words_listed = sb.tile([P, SLOTS], U16, name="v_words_listed", tag="behind_dq", align_bytes=64)
        nc.vector.tensor_copy(v_words_listed[:], v_words[:].indirect(offsets[:]))
        nc.vector.quantize_mx(
            gout_codes[:].bitcast(FP8X4), gout_scales[:], gout_bf[:].rearrange("p w j -> p (w j)")
        )
        v_bytes_low = sb.tile([P, half], U8, name="v_bytes_low", tag="behind_q", align_bytes=64)
        c0_half(0, v_bytes_low)

        soft = f32_tile("soft", SLOTS)
        soft_sum = f32_tile("soft_sum", 1)
        minus_shift = f32_tile("minus_shift", 1)
        e = f32_tile("e", SLOTS)
        nc.scalar.activation(soft[:], a[:], ACT.Exp, scale=1.0 / SOFTEN, accum_out=soft_sum[:])
        nc.scalar.activation(
            minus_shift[:], soft_sum[:].bitcast(U32), ACT.Copy,
            scale=-SOFTEN * math.log(2.0) / 2.0**23,
            bias=SOFTEN * math.log(2.0) * (127 + math.log2(SLOTS) / 2),
        )

        sums = f32_tile("sums", 2 * GROUPS)
        nc.vector.tensor_reduce(sums[:, 0:GROUPS], in_eights(a[:]), AX.X, ALU.add)
        nc.scalar.activation(e[:], a[:], ACT.Exp, bias=minus_shift[:])
        nc.vector.tensor_reduce(sums[:, GROUPS : 2 * GROUPS], in_eights(ta[:]), AX.X, ALU.add)
        block_sums = sb.tile([P, 2 * BLOCKS], F32, name="block_sums", tag="behind_diff", align_bytes=64)
        nc.vector.tensor_reduce(block_sums[:], in_eights(sums[:]), AX.X, ALU.add)
        diff = f32_tile("diff", 2 * GROUPS)
        nc.vector.scalar_tensor_tensor(
            in_eights(diff[:]), spread(block_sums[:], FAN), -1.0 / FAN, in_eights(sums[:]), ALU.mult, ALU.add
        )
        v_bytes_high = sb.tile([P, half], U8, name="v_bytes_high", tag="behind_diff", align_bytes=64)
        c0_half(half, v_bytes_high)
        th = f32_tile("th", GROUPS)
        nc.scalar.activation(th[:], diff[:, 0:GROUPS], ACT.Tanh, scale=steep16[:])
        gates = f32_tile("gates", 2 * GROUPS)
        shut = gates[:, 0:GROUPS]
        nc.scalar.activation(shut, th[:], ACT.Identity, scale=minus_steep16[:], bias=steep16[:])
        nc.scalar.activation(gates[:, GROUPS : 2 * GROUPS], th[:], ACT.Identity, scale=steep16[:], bias=steep16[:])

        p = f32_tile("p", SLOTS)
        z = f32_tile("z", 1)
        nc.vector.scalar_tensor_tensor(
            in_eights(p[:]), spread(th[:], FAN), 1.0, in_eights(e[:]), ALU.add, ALU.mult, accum_out=z[:]
        )
        rz = f32_tile("rz", 1)
        nc.vector.reciprocal(rz[:], z[:])
        p_sums_and_k = f32_tile("p_sums_and_k", 2 * GROUPS)
        k_rz = p_sums_and_k[:, GROUPS : 2 * GROUPS]
        nc.vector.tensor_reduce(p_sums_and_k[:, 0:GROUPS], in_eights(p[:]), AX.X, ALU.add)
        nc.vector.scalar_tensor_tensor(k_rz, diff[:, GROUPS : 2 * GROUPS], rz[:], shut, ALU.mult, ALU.mult)
        p_c0 = f32_tile("p_c0", SLOTS)
        p_c0_sum = f32_tile("p_c0_sum", 1)
        nc.vector.scalar_tensor_tensor(p_c0[:], c0[:], GAIN, p[:], ALU.mult, ALU.mult, accum_out=p_c0_sum[:])
        c0_mean = f32_tile("c0_mean", 1)
        nc.scalar.activation(c0_mean[:], p_c0_sum[:], ACT.Copy, scale=rz[:])
        u_rz = f32_tile("u_rz", SLOTS)
        nc.vector.scalar_tensor_tensor(
            in_eights(u_rz[:]), in_eights(ta[:]), rz[:], spread(k_rz, FAN), ALU.mult, ALU.add
        )
        minus_pc = f32_tile("minus_pc", SLOTS)
        nc.vector.scalar_tensor_tensor(minus_pc[:], p[:], c0_mean[:], p_c0[:], ALU.mult, ALU.subtract)
        wu = f32_tile("wu", SLOTS)
        tau = f32_tile("tau", 1)
        nc.vector.scalar_tensor_tensor(wu[:], p[:], 1.0, u_rz[:], ALU.mult, ALU.mult, accum_out=tau[:])
        tau_rz = f32_tile("tau_rz", 1)
        nc.scalar.activation(tau_rz[:], tau[:], ACT.Copy, scale=rz[:])
        minus_pc_sums = f32_tile("minus_pc_sums", GROUPS)
        nc.vector.tensor_reduce(minus_pc_sums[:], in_eights(minus_pc[:]), AX.X, ALU.add)
        minus_wcu = f32_tile("minus_wcu", SLOTS)
        minus_nu = f32_tile("minus_nu", 1)
        nc.vector.scalar_tensor_tensor(
            minus_wcu[:], u_rz[:], tau_rz[:], minus_pc[:], ALU.subtract, ALU.mult, accum_out=minus_nu[:]
        )
        minus_nu_rz = f32_tile("minus_nu_rz", 1)
        nc.scalar.activation(minus_nu_rz[:], minus_nu[:], ACT.Copy, scale=rz[:])

        gated = f32_tile("gated", 2 * GROUPS)
        nc.vector.tensor_tensor(gated[:], p_sums_and_k[:], gates[:], ALU.mult)
        minus_wcu_sums = f32_tile("minus_wcu_sums", GROUPS)
        nc.vector.tensor_reduce(minus_wcu_sums[:], in_eights(minus_wcu[:]), AX.X, ALU.add)
        x_wc = f32_tile("x_wc", GROUPS)
        nc.vector.tensor_tensor(x_wc[:], minus_pc_sums[:], gated[:, GROUPS : 2 * GROUPS], ALU.mult)
        minus_x_wcu = f32_tile("minus_x_wcu", GROUPS)
        nc.vector.tensor_tensor(minus_x_wcu[:], minus_wcu_sums[:], shut, ALU.mult)
        x_rest = f32_tile("x_rest", GROUPS)
        nc.vector.scalar_tensor_tensor(x_rest[:], gated[:, 0:GROUPS], minus_nu_rz[:], x_wc[:], ALU.mult, ALU.add)
        f = f32_tile("f", SLOTS)

        def f_piece(piece):
            slots = slice(F_EDGES[piece], F_EDGES[piece + 1])
            nc.vector.scalar_tensor_tensor(
                f[:, slots], p[:, slots], minus_nu_rz[:], minus_wcu[:, slots], ALU.mult, ALU.subtract
            )

        f_piece(0)
        x = f32_tile("x", GROUPS)
        nc.vector.tensor_tensor(x[:], x_rest[:], minus_x_wcu[:], ALU.subtract)
        f_piece(1)
        x_block_sums = f32_tile("x_block_sums", BLOCKS)
        nc.vector.tensor_reduce(x_block_sums[:], in_eights(x[:]), AX.X, ALU.add)
        f_piece(2)
        r = f32_tile("r", SLOTS)
        nc.vector.scalar_tensor_tensor(
            in_eights(r[:]), spread(x_block_sums[:], FAN * FAN), -1.0 / FAN, spread(x[:], FAN), ALU.mult, ALU.add
        )

        nc.vector.tensor_tensor(window[:].indirect(offsets[:]), f[:], r[:], ALU.add)
        for piece in range(len(OUT_EDGES) - 1):
            cols = slice(OUT_EDGES[piece], OUT_EDGES[piece + 1])
            result = f32_tile("result%d" % piece, OUT_EDGES[piece + 1] - OUT_EDGES[piece])
            nc.vector.tensor_tensor(result[:], window[:, cols], base_sb[:, cols], ALU.add)
            nc.sync.dma_start(out[:, cols], result[:])
